import numpy as np
import ml_dtypes


def mxq(x, axis, fmt="e4m3"):
    dtype, down = {"e4m3": (ml_dtypes.float8_e4m3fn, 7), "e5m2": (ml_dtypes.float8_e5m2, 14)}[fmt]
    v = np.moveaxis(np.asarray(x, np.float32).astype(ml_dtypes.bfloat16).astype(np.float64), axis, -1)
    blocks = v.reshape(v.shape[:-1] + (-1, 32))
    amax = np.abs(blocks).max(-1, keepdims=True)
    byte = np.maximum(np.where(amax > 0, np.frexp(amax)[1] - 1 + 127, 0) - down, 1)
    scale = np.exp2(byte - 127.0)
    codes = (blocks / scale).astype(np.float32).astype(dtype).astype(np.float64)
    return np.moveaxis((codes * scale).reshape(v.shape), -1, axis)


WIDE = False


def mx_kscale(k):
    if not WIDE:
        return np.ones(k)
    levels = np.array([10, -10, 5, -5, 0])
    if k % 512:
        return np.exp2(np.random.permutation(np.resize(levels, k // 32))).repeat(32)
    a = np.empty((k // 512, 16))
    for p in range(k // 512):
        a[p, :8] = np.random.permutation(np.resize(levels, 8))
        for g in range(8):
            far = levels[np.abs(levels - a[p, g]) >= 10]
            a[p, g + 8] = far[np.random.randint(len(far))]
    return np.exp2(a.ravel()).repeat(32)


def f64(x):
    return np.asarray(x).astype(np.float64)


def striped8(idx):
    return np.asarray(idx).reshape(8, -1, 16).transpose(0, 2, 1).reshape(128, -1).astype(np.uint16)


def unstriped8(offs):
    return offs.reshape(8, 16, -1).transpose(0, 2, 1).reshape(8, -1).astype(np.int64)


def pick8(x, idx, run):
    r = np.arange(len(x))
    return x[r[:, None], idx[r % (8 * run) // run]]


E2M1 = np.array([0.0, 0.5, 1.0, 1.5, 2.0, 3.0, 4.0, 6.0, -0.0, -0.5, -1.0, -1.5, -2.0, -3.0, -4.0, -6.0])


def pack_weight(w, fmt):
    k, n = w.shape
    w = f64(np.asarray(w, np.float32).astype(ml_dtypes.bfloat16)).reshape(k // 32, 32, n)
    amax = np.abs(w).max(1)
    if fmt == "e4m3":
        byte = np.frexp(amax)[1] - 1 + 127 - 7
    else:
        mant, ex = np.frexp(amax / 6.0)
        byte = np.where(mant > 0.5, ex, ex - 1) + 127
    byte = np.clip(np.where(amax > 0, byte, 1), 1, 254)
    scaled = (w * np.exp2(127.0 - byte)[:, None, :]).reshape(k, n).astype(np.float32)
    by_word = np.ascontiguousarray(scaled.reshape(k // 512, 128, 4, n).transpose(0, 1, 3, 2))
    if fmt == "e4m3":
        words = by_word.astype(ml_dtypes.float8_e4m3fn).view(np.uint8)
    else:
        c = by_word.astype(ml_dtypes.float4_e2m1fn).view(np.uint8) & 0xF
        words = (c[..., 0::2] | (c[..., 1::2] << 4)).reshape(k // 512, 128, 2 * n)
    return np.ascontiguousarray(words), np.ascontiguousarray(byte.astype(np.uint8).reshape(k // 512, 16, n))


def unpack_weight(words, scales, fmt):
    g, _, n = scales.shape
    words = np.ascontiguousarray(words).reshape(g, 128, n, -1)
    if fmt == "e4m3":
        vals = words.view(ml_dtypes.float8_e4m3fn).astype(np.float64)
    else:
        nib = np.empty((g, 128, n, 4), np.uint8)
        nib[..., 0::2] = words & 0xF
        nib[..., 1::2] = words >> 4
        vals = E2M1[nib]
    vals = vals * np.repeat(np.exp2(scales.astype(np.float64) - 127.0), 8, axis=1)[..., None]
    return vals.transpose(0, 1, 3, 2).reshape(g * 512, n)


D, T, I, Q = 512, 1024, 512, 128


def setup_inputs():
    n = np.random.standard_normal
    idx = np.stack([np.random.permutation(T)[:I] for _ in range(8)])
    idx2 = np.stack([np.random.permutation(T)[:I] for _ in range(8)])
    idx3 = np.stack([np.random.permutation(T)[:I] for _ in range(8)])
    idx4 = np.stack([np.random.permutation(T)[:I] for _ in range(8)])
    fd = mx_kscale(D)
    keysp = pack_weight(n((D, T)) / fd[:, None], "e2m1")
    return {
        "query": (n((D, Q)) * 0.9 / np.sqrt(D) * fd[:, None]).astype(np.float32),
        "keys_words": keysp[0],
        "keys_scales": keysp[1],
        "lam": (np.random.uniform(0.7, 1.3, (Q, 1))).astype(np.float32),
        "old": (1.0 * n((Q, T))).astype(np.float32),
        "offs": striped8(idx),
        "offs2": striped8(idx2),
        "offs3": striped8(idx3),
        "offs4": striped8(idx4),
    }


def reference(query, keys_words, keys_scales, lam, old, offs, offs2, offs3, offs4):
    idx = unstriped8(offs)
    idx2 = unstriped8(offs2)
    idx3 = unstriped8(offs3)
    idx4 = unstriped8(offs4)
    keysu = unpack_weight(keys_words, keys_scales, "e2m1")
    queryq = mxq(f64(query), 0, "e4m3")
    a = queryq.T @ keysu
    w = pick8(a, idx, 16) * f64(lam) - np.abs(pick8(a, idx2, 16) - pick8(a, idx3, 16))
    f1 = np.zeros((Q, T))
    f1[np.arange(Q)[:, None], idx4[np.arange(Q) % 128 // 16]] = w
    y = np.maximum(f1, f64(old)) + f64(old) * 0.25
    return y

@@ -1,0 +1,147 @@
+from contextlib import ExitStack
+
+import concourse.mybir as mybir
+
+D, T, SLOTS, Q = 512, 1024, 512, 128
+P = 128
+PACK = 4
+BANK = 512
+HALF = SLOTS // 2
+PER_COLUMN = 16
+
+F32 = mybir.dt.float32
+BF16 = mybir.dt.bfloat16
+U32 = mybir.dt.uint32
+I32 = mybir.dt.int32
+U16 = mybir.dt.uint16
+U8 = mybir.dt.uint8
+FP8X4 = mybir.dt.float8_e4m3fn_x4
+FP4X4 = mybir.dt.float4_e2m1fn_x4
+ALU = mybir.AluOpType
+ACT = mybir.ActivationFunctionType
+
+FLOPS = 2 * D * T * Q
+OUT_CHUNKS = (384, 256, 256, 128)
+SCORE_CHUNKS = (512, 256, 128, 128)
+
+
+def tile_attend_betweentwo_lean_largerput_heads_kernel(
+    tc, query, keys_words, keys_scales, lam, old, offs, offs2, offs3, offs4, out
+):
+    nc = tc.nc
+    with ExitStack() as ctx:
+        held = ctx.enter_context(tc.tile_pool(name="held", bufs=1))
+        psum = ctx.enter_context(tc.psum_pool(name="psum", bufs=1))
+
+        k_scales = held.tile([P, T], U8, name="k_scales", align_bytes=64)
+        nc.vector.memset(k_scales[:].bitcast(I32), 0)
+        for quad in range(4):
+            nc.scalar.dma_start(
+                out=k_scales[32 * quad : 32 * quad + 4, :].bitcast(I32),
+                in_=keys_scales[0, 4 * quad : 4 * quad + 4, :].bitcast(I32),
+            )
+
+        q_raw = held.tile([P, PACK, Q], F32, name="q_raw")
+        nc.sync.dma_start(out=q_raw[:], in_=query.rearrange("(p j) q -> p j q", j=PACK))
+        k_words = held.tile([P, 2 * T], U8, name="k_words", align_bytes=64)
+        nc.sync.dma_start(out=k_words[:].bitcast(I32), in_=keys_words[0].bitcast(I32))
+        third = held.tile([P, SLOTS // PER_COLUMN], U16, name="third")
+        nc.sync.dma_start(third[:], offs3)
+        second = held.tile([P, SLOTS // PER_COLUMN], U16, name="second")
+        nc.sync.dma_start(second[:], offs2)
+        first = held.tile([P, SLOTS // PER_COLUMN], U16, name="first")
+        nc.sync.dma_start(first[:], offs)
+        lam_col = held.tile([P, 1], F32, name="lam_col")
+        nc.sync.dma_start(out=lam_col[:], in_=lam)
+        places = held.tile([P, SLOTS // PER_COLUMN], U16, name="places")
+        nc.sync.dma_start(places[:], offs4)
+        old_sb = held.tile([P, T], F32, name="old_sb")
+        nc.sync.dma_start(out=old_sb[:], in_=old)
+
+        placed = held.tile([P, T], F32, name="placed")
+        nc.vector.memset(placed[:], 0.0)
+
+        q_grouped = held.tile([P, Q, PACK], BF16, name="q_grouped", align_bytes=64)
+        nc.vector.tensor_copy(out=q_grouped[:], in_=q_raw[:].rearrange("p j q -> p q j"))
+        q_codes = held.tile([P, Q], U32, name="q_codes", align_bytes=64)
+        q_scales = held.tile([P, Q], U8, name="q_scales", align_bytes=64)
+        nc.vector.quantize_mx(
+            out=q_codes[:].bitcast(FP8X4),
+            scales=q_scales[:],
+            in_=q_grouped[:].rearrange("p q j -> p (q j)"),
+        )
+
+        scores = held.tile([P, T], F32, name="scores")
+        start = 0
+        for b, width in enumerate(SCORE_CHUNKS):
+            cols = slice(start, start + width)
+            start = start + width
+            bank = psum.tile([P, width], F32, name="bank%d" % b)
+            nc.tensor.matmul_mx(
+                out=bank[:],
+                lhsT=q_codes[:].bitcast(FP8X4),
+                lhsT_scale=q_scales[:],
+                rhs=k_words[:, 2 * cols.start : 2 * cols.stop].bitcast(FP4X4),
+                rhs_scale=k_scales[:, cols],
+                start=True,
+                stop=True,
+            )
+            if b % 2 == 0:
+                nc.scalar.activation(scores[:, cols], bank[:], ACT.Copy)
+            else:
+                nc.vector.tensor_copy(out=scores[:, cols], in_=bank[:])
+
+        def listed(tile, offsets, h):
+            cols = HALF // PER_COLUMN
+            return tile[:].indirect(offsets[:, h * cols : (h + 1) * cols])
+
+        def work(name):
+            return [held.tile([P, HALF], F32, name="%s%d" % (name, h)) for h in range(2)]
+
+        a_second, a_third, minus_size, leaning = (
+            work("a_second"), work("a_third"), work("minus_size"), work("leaning")
+        )
+        a_first = held.tile([P, HALF], F32, name="a_first")
+        diff = held.tile([P, HALF], F32, name="diff")
+        size = held.tile([P, HALF], F32, name="size")
+
+        nc.scalar.activation(a_third[0][:], listed(scores, third, 0), ACT.Copy)
+        nc.vector.tensor_copy(a_second[0][:], listed(scores, second, 0))
+        nc.scalar.activation(a_first[:], listed(scores, first, 0), ACT.Copy)
+        nc.vector.tensor_copy(a_second[1][:], listed(scores, second, 1))
+        nc.scalar.activation(a_third[1][:], listed(scores, third, 1), ACT.Copy)
+        nc.vector.tensor_tensor(diff[:], a_second[0][:], a_third[0][:], ALU.subtract)
+        nc.scalar.activation(leaning[0][:], a_first[:], ACT.Copy, scale=lam_col[:])
+        nc.vector.scalar_tensor_tensor(minus_size[0][:], diff[:], -1.0, diff[:], ALU.mult, ALU.min)
+        nc.vector.tensor_tensor(diff[:], a_second[1][:], a_third[1][:], ALU.subtract)
+        nc.vector.tensor_tensor(listed(placed, places, 0), leaning[0][:], minus_size[0][:], ALU.add)
+        nc.scalar.activation(a_first[:], listed(scores, first, 1), ACT.Copy)
+        nc.scalar.activation(size[:], diff[:], ACT.Abs)
+        nc.scalar.activation(leaning[1][:], a_first[:], ACT.Copy, scale=lam_col[:])
+        nc.scalar.activation(minus_size[1][:], size[:], ACT.Copy, scale=-1.0)
+        nc.vector.tensor_tensor(listed(placed, places, 1), leaning[1][:], minus_size[1][:], ALU.add)
+
+        larger = held.tile([P, T], F32, name="larger")
+        result = held.tile([P, T], F32, name="result")
+        spans = []
+        start = 0
+        for width in OUT_CHUNKS:
+            spans.append(slice(start, start + width))
+            start = start + width
+
+        def take_larger(cols):
+            nc.vector.tensor_tensor(larger[:, cols], placed[:, cols], old_sb[:, cols], ALU.max)
+
+        def finish(c):
+            cols = spans[c]
+            nc.vector.scalar_tensor_tensor(
+                result[:, cols], old_sb[:, cols], 0.25, larger[:, cols], ALU.mult, ALU.add
+            )
+            queue = nc.sync if c % 2 == 0 else nc.scalar
+            queue.dma_start(out=out[:, cols], in_=result[:, cols])
+
+        take_larger(spans[0])
+        for c in range(1, len(spans)):
+            take_larger(spans[c])
+            finish(c - 1)
+        finish(len(spans) - 1)

@@ -1,6 +1,7 @@
 from contextlib import ExitStack
 
 import concourse.mybir as mybir
+from concourse.masks import make_identity
 
 D, T, SLOTS, Q = 512, 1024, 512, 128
 P = 128
@@ -62,7 +63,10 @@ def tile_attend_betweentwo_lean_largerput_heads_kernel(
         nc.vector.memset(placed[:], 0.0)
 
         q_grouped = held.tile([P, Q, PACK], BF16, name="q_grouped", align_bytes=64)
-        nc.vector.tensor_copy(out=q_grouped[:], in_=q_raw[:].rearrange("p j q -> p q j"))
+        nc.vector.tensor_copy(
+            out=q_grouped[:].rearrange("p (c i) j -> p c j i", i=4),
+            in_=q_raw[:].rearrange("p j (c i) -> p c j i", i=4),
+        )
         q_codes = held.tile([P, Q], U32, name="q_codes", align_bytes=64)
         q_scales = held.tile([P, Q], U8, name="q_scales", align_bytes=64)
         nc.vector.quantize_mx(
@@ -102,46 +106,58 @@ def tile_attend_betweentwo_lean_largerput_heads_kernel(
             work("a_second"), work("a_third"), work("minus_size"), work("leaning")
         )
         a_first = held.tile([P, HALF], F32, name="a_first")
-        diff = held.tile([P, HALF], F32, name="diff")
-        size = held.tile([P, HALF], F32, name="size")
+        diff = work("diff")
+        size = held.tile([P, HALF], F32, name="size", tag="late")
 
         nc.scalar.activation(a_third[0][:], listed(scores, third, 0), ACT.Copy)
         nc.vector.tensor_copy(a_second[0][:], listed(scores, second, 0))
         nc.scalar.activation(a_first[:], listed(scores, first, 0), ACT.Copy)
         nc.vector.tensor_copy(a_second[1][:], listed(scores, second, 1))
         nc.scalar.activation(a_third[1][:], listed(scores, third, 1), ACT.Copy)
-        nc.vector.tensor_tensor(diff[:], a_second[0][:], a_third[0][:], ALU.subtract)
+        nc.vector.tensor_tensor(diff[0][:], a_second[0][:], a_third[0][:], ALU.subtract)
         nc.scalar.activation(leaning[0][:], a_first[:], ACT.Copy, scale=lam_col[:])
-        nc.vector.scalar_tensor_tensor(minus_size[0][:], diff[:], -1.0, diff[:], ALU.mult, ALU.min)
-        nc.vector.tensor_tensor(diff[:], a_second[1][:], a_third[1][:], ALU.subtract)
+        nc.vector.scalar_tensor_tensor(minus_size[0][:], diff[0][:], -1.0, diff[0][:], ALU.mult, ALU.min)
+        nc.vector.tensor_tensor(diff[1][:], a_second[1][:], a_third[1][:], ALU.subtract)
         nc.vector.tensor_tensor(listed(placed, places, 0), leaning[0][:], minus_size[0][:], ALU.add)
         nc.scalar.activation(a_first[:], listed(scores, first, 1), ACT.Copy)
-        nc.scalar.activation(size[:], diff[:], ACT.Abs)
+        nc.scalar.activation(size[:], diff[1][:], ACT.Abs)
         nc.scalar.activation(leaning[1][:], a_first[:], ACT.Copy, scale=lam_col[:])
         nc.scalar.activation(minus_size[1][:], size[:], ACT.Copy, scale=-1.0)
         nc.vector.tensor_tensor(listed(placed, places, 1), leaning[1][:], minus_size[1][:], ALU.add)
 
-        larger = held.tile([P, T], F32, name="larger")
+        identity = held.tile([P, P], F32, name="identity")
+        make_identity(nc, identity[:])
+        old_turned = held.tile([P, T], F32, name="old_turned", tag="late")
+        old_back = []
+        for b, factor in enumerate((1.0, 1.25)):
+            turned = psum.tile([P, BANK], F32, name="turned%d" % b)
+            back = psum.tile([P, BANK], F32, name="back%d" % b)
+            blocks = [slice(P * i, P * (i + 1)) for i in range(BANK // P)]
+            half = slice(BANK * b, BANK * (b + 1))
+            for blk in blocks:
+                nc.tensor.transpose(turned[:, blk], old_sb[:, half][:, blk], identity[:])
+            nc.scalar.activation(old_turned[:, half], turned[:], ACT.Copy, scale=factor)
+            for blk in blocks:
+                nc.tensor.transpose(back[:, blk], old_turned[:, half][:, blk], identity[:])
+            old_back.append(back)
+
+        step = held.tile([P, T], F32, name="step")
         result = held.tile([P, T], F32, name="result")
-        spans = []
-        start = 0
-        for width in OUT_CHUNKS:
-            spans.append(slice(start, start + width))
-            start = start + width
-
-        def take_larger(cols):
-            nc.vector.tensor_tensor(larger[:, cols], placed[:, cols], old_sb[:, cols], ALU.max)
-
-        def finish(c):
-            cols = spans[c]
+        W = 256
+        for c in range(2):
+            cols = slice(BANK + W * c, BANK + W * (c + 1))
+            nc.gpsimd.tensor_tensor(step[:, cols], placed[:, cols], old_sb[:, cols], ALU.subtract)
+        for c in range(2):
+            cols = slice(W * c, W * (c + 1))
+            nc.vector.tensor_tensor(step[:, cols], placed[:, cols], old_back[0][:, cols], ALU.max)
+        for c in range(2):
+            cols = slice(W * c, W * (c + 1))
             nc.vector.scalar_tensor_tensor(
-                result[:, cols], old_sb[:, cols], 0.25, larger[:, cols], ALU.mult, ALU.add
+                result[:, cols], old_back[0][:, cols], 0.25, step[:, cols], ALU.mult, ALU.add
             )
-            queue = nc.sync if c % 2 == 0 else nc.scalar
-            queue.dma_start(out=out[:, cols], in_=result[:, cols])
-
-        take_larger(spans[0])
-        for c in range(1, len(spans)):
-            take_larger(spans[c])
-            finish(c - 1)
-        finish(len(spans) - 1)
+            nc.sync.dma_start(out=out[:, cols], in_=result[:, cols])
+            high = slice(BANK + W * c, BANK + W * (c + 1))
+            nc.vector.scalar_tensor_tensor(
+                result[:, high], step[:, high], 0.0, old_back[1][:, cols], ALU.max, ALU.add
+            )
+            nc.scalar.dma_start(out=out[:, high], in_=result[:, high])

from contextlib import ExitStack

import concourse.mybir as mybir
from concourse.masks import make_identity

D, T, SLOTS, Q = 512, 1024, 512, 128
P = 128
PACK = 4
BANK = 512
HALF = SLOTS // 2
PER_COLUMN = 16

F32 = mybir.dt.float32
BF16 = mybir.dt.bfloat16
U32 = mybir.dt.uint32
I32 = mybir.dt.int32
U16 = mybir.dt.uint16
U8 = mybir.dt.uint8
FP8X4 = mybir.dt.float8_e4m3fn_x4
FP4X4 = mybir.dt.float4_e2m1fn_x4
ALU = mybir.AluOpType
ACT = mybir.ActivationFunctionType

FLOPS = 2 * D * T * Q
OUT_CHUNKS = (384, 256, 256, 128)
SCORE_CHUNKS = (512, 256, 128, 128)


def tile_attend_betweentwo_lean_largerput_heads_kernel(
    tc, query, keys_words, keys_scales, lam, old, offs, offs2, offs3, offs4, out
):
    nc = tc.nc
    with ExitStack() as ctx:
        held = ctx.enter_context(tc.tile_pool(name="held", bufs=1))
        psum = ctx.enter_context(tc.psum_pool(name="psum", bufs=1))

        k_scales = held.tile([P, T], U8, name="k_scales", align_bytes=64)
        nc.vector.memset(k_scales[:].bitcast(I32), 0)
        for quad in range(4):
            nc.scalar.dma_start(
                out=k_scales[32 * quad : 32 * quad + 4, :].bitcast(I32),
                in_=keys_scales[0, 4 * quad : 4 * quad + 4, :].bitcast(I32),
            )

        q_raw = held.tile([P, PACK, Q], F32, name="q_raw")
        nc.sync.dma_start(out=q_raw[:], in_=query.rearrange("(p j) q -> p j q", j=PACK))
        k_words = held.tile([P, 2 * T], U8, name="k_words", align_bytes=64)
        nc.sync.dma_start(out=k_words[:].bitcast(I32), in_=keys_words[0].bitcast(I32))
        third = held.tile([P, SLOTS // PER_COLUMN], U16, name="third")
        nc.sync.dma_start(third[:], offs3)
        second = held.tile([P, SLOTS // PER_COLUMN], U16, name="second")
        nc.sync.dma_start(second[:], offs2)
        first = held.tile([P, SLOTS // PER_COLUMN], U16, name="first")
        nc.sync.dma_start(first[:], offs)
        lam_col = held.tile([P, 1], F32, name="lam_col")
        nc.sync.dma_start(out=lam_col[:], in_=lam)
        places = held.tile([P, SLOTS // PER_COLUMN], U16, name="places")
        nc.sync.dma_start(places[:], offs4)
        old_sb = held.tile([P, T], F32, name="old_sb")
        nc.sync.dma_start(out=old_sb[:], in_=old)

        placed = held.tile([P, T], F32, name="placed")
        nc.vector.memset(placed[:], 0.0)

        q_grouped = held.tile([P, Q, PACK], BF16, name="q_grouped", align_bytes=64)
        nc.vector.tensor_copy(
            out=q_grouped[:].rearrange("p (c i) j -> p c j i", i=4),
            in_=q_raw[:].rearrange("p j (c i) -> p c j i", i=4),
        )
        q_codes = held.tile([P, Q], U32, name="q_codes", align_bytes=64)
        q_scales = held.tile([P, Q], U8, name="q_scales", align_bytes=64)
        nc.vector.quantize_mx(
            out=q_codes[:].bitcast(FP8X4),
            scales=q_scales[:],
            in_=q_grouped[:].rearrange("p q j -> p (q j)"),
        )

        scores = held.tile([P, T], F32, name="scores")
        start = 0
        for b, width in enumerate(SCORE_CHUNKS):
            cols = slice(start, start + width)
            start = start + width
            bank = psum.tile([P, width], F32, name="bank%d" % b)
            nc.tensor.matmul_mx(
                out=bank[:],
                lhsT=q_codes[:].bitcast(FP8X4),
                lhsT_scale=q_scales[:],
                rhs=k_words[:, 2 * cols.start : 2 * cols.stop].bitcast(FP4X4),
                rhs_scale=k_scales[:, cols],
                start=True,
                stop=True,
            )
            if b % 2 == 0:
                nc.scalar.activation(scores[:, cols], bank[:], ACT.Copy)
            else:
                nc.vector.tensor_copy(out=scores[:, cols], in_=bank[:])

        def listed(tile, offsets, h):
            cols = HALF // PER_COLUMN
            return tile[:].indirect(offsets[:, h * cols : (h + 1) * cols])

        def work(name):
            return [held.tile([P, HALF], F32, name="%s%d" % (name, h)) for h in range(2)]

        a_second, a_third, minus_size, leaning = (
            work("a_second"), work("a_third"), work("minus_size"), work("leaning")
        )
        a_first = held.tile([P, HALF], F32, name="a_first")
        diff = work("diff")
        size = held.tile([P, HALF], F32, name="size", tag="late")

        nc.scalar.activation(a_third[0][:], listed(scores, third, 0), ACT.Copy)
        nc.vector.tensor_copy(a_second[0][:], listed(scores, second, 0))
        nc.scalar.activation(a_first[:], listed(scores, first, 0), ACT.Copy)
        nc.vector.tensor_copy(a_second[1][:], listed(scores, second, 1))
        nc.scalar.activation(a_third[1][:], listed(scores, third, 1), ACT.Copy)
        nc.vector.tensor_tensor(diff[0][:], a_second[0][:], a_third[0][:], ALU.subtract)
        nc.scalar.activation(leaning[0][:], a_first[:], ACT.Copy, scale=lam_col[:])
        nc.vector.scalar_tensor_tensor(minus_size[0][:], diff[0][:], -1.0, diff[0][:], ALU.mult, ALU.min)
        nc.vector.tensor_tensor(diff[1][:], a_second[1][:], a_third[1][:], ALU.subtract)
        nc.vector.tensor_tensor(listed(placed, places, 0), leaning[0][:], minus_size[0][:], ALU.add)
        nc.scalar.activation(a_first[:], listed(scores, first, 1), ACT.Copy)
        nc.scalar.activation(size[:], diff[1][:], ACT.Abs)
        nc.scalar.activation(leaning[1][:], a_first[:], ACT.Copy, scale=lam_col[:])
        nc.scalar.activation(minus_size[1][:], size[:], ACT.Copy, scale=-1.0)
        nc.vector.tensor_tensor(listed(placed, places, 1), leaning[1][:], minus_size[1][:], ALU.add)

        identity = held.tile([P, P], F32, name="identity")
        make_identity(nc, identity[:])
        old_turned = held.tile([P, T], F32, name="old_turned", tag="late")
        old_back = []
        for b, factor in enumerate((1.0, 1.25)):
            turned = psum.tile([P, BANK], F32, name="turned%d" % b)
            back = psum.tile([P, BANK], F32, name="back%d" % b)
            blocks = [slice(P * i, P * (i + 1)) for i in range(BANK // P)]
            half = slice(BANK * b, BANK * (b + 1))
            for blk in blocks:
                nc.tensor.transpose(turned[:, blk], old_sb[:, half][:, blk], identity[:])
            nc.scalar.activation(old_turned[:, half], turned[:], ACT.Copy, scale=factor)
            for blk in blocks:
                nc.tensor.transpose(back[:, blk], old_turned[:, half][:, blk], identity[:])
            old_back.append(back)

        step = held.tile([P, T], F32, name="step")
        result = held.tile([P, T], F32, name="result")
        W = 256
        for c in range(2):
            cols = slice(BANK + W * c, BANK + W * (c + 1))
            nc.gpsimd.tensor_tensor(step[:, cols], placed[:, cols], old_sb[:, cols], ALU.subtract)
        for c in range(2):
            cols = slice(W * c, W * (c + 1))
            nc.vector.tensor_tensor(step[:, cols], placed[:, cols], old_back[0][:, cols], ALU.max)
        for c in range(2):
            cols = slice(W * c, W * (c + 1))
            nc.vector.scalar_tensor_tensor(
                result[:, cols], old_back[0][:, cols], 0.25, step[:, cols], ALU.mult, ALU.add
            )
            nc.sync.dma_start(out=out[:, cols], in_=result[:, cols])
            high = slice(BANK + W * c, BANK + W * (c + 1))
            nc.vector.scalar_tensor_tensor(
                result[:, high], step[:, high], 0.0, old_back[1][:, cols], ALU.max, ALU.add
            )
            nc.scalar.dma_start(out=out[:, high], in_=result[:, high])
